import numpy as np
import ml_dtypes

BF16 = ml_dtypes.bfloat16


def bf(x):
    return np.asarray(x, np.float32).astype(BF16)


def f32(x):
    return np.asarray(x, np.float32)


def f64(x):
    return np.asarray(x).astype(np.float64)


def striped(idx):
    return np.tile(idx.reshape(-1, 16).T, (8, 1))


S, K, M, N, D, V = 2048, 256, 128, 1536, 4, 384


def setup_inputs():
    return {"table": bf(np.random.standard_normal((K, S))), "w": bf(np.random.standard_normal((D, K, M)) / np.sqrt(D * K)), "r": f32(np.random.standard_normal((M, V))), "offs": striped(np.random.permutation(np.tile(np.arange(S), 2))[:N])}


def reference(table, w, r, offs):
    idx = offs[:16].T.reshape(-1)
    x = f64(table)[:, idx]
    y = sum(f64(w)[t].T @ x[:, t * V : (t + 1) * V] for t in range(D))
    return y + f64(r)

@@ -1,0 +1,54 @@
+import concourse.mybir as mybir
+
+BF16, F32, U16 = mybir.dt.bfloat16, mybir.dt.float32, mybir.dt.uint16
+
+P = 128
+S = 2048
+K = 256
+M = 128
+RELATIONS = 4
+V = 384
+N = RELATIONS * V
+BLOCKS = K // P
+COLS = V // 16
+
+FLOPS = 2 * K * M * N
+
+
+def tile_gather_matmul_kernel(tc, table, w, r, offs, out):
+    nc = tc.nc
+    with (
+        tc.tile_pool(name="held", bufs=1) as held,
+        tc.psum_pool(name="psum", bufs=1) as psum,
+    ):
+        offsets = held.tile([P, N // 16], U16, name="offsets")
+        nc.sync.dma_start(offsets[:], offs)
+
+        windows = []
+        weights = []
+        for b in range(BLOCKS):
+            rows = slice(b * P, (b + 1) * P)
+            window = held.tile([P, S], BF16, name="window%d" % b)
+            nc.sync.dma_start(window[:], table[rows, :])
+            windows.append(window)
+            weight = held.tile([P, RELATIONS, M], BF16, name="weight%d" % b)
+            nc.scalar.dma_start(weight[:], w[:, rows, :].rearrange("t p m -> p t m"))
+            weights.append(weight)
+
+        own = held.tile([M, V], F32, name="own")
+        nc.gpsimd.dma_start(own[:], r)
+
+        bank = psum.tile([M, V], F32, name="bank")
+        for b in range(BLOCKS):
+            for t in range(RELATIONS):
+                nc.tensor.matmul(
+                    bank[:],
+                    weights[b][:, t, :],
+                    windows[b][:].indirect(offsets[:, t * COLS : (t + 1) * COLS]),
+                    start=(b == 0 and t == 0),
+                    stop=(b == BLOCKS - 1 and t == RELATIONS - 1),
+                )
+
+        result = held.tile([M, V], F32, name="result")
+        nc.vector.tensor_tensor(result[:], bank[:], own[:], mybir.AluOpType.add)
+        nc.sync.dma_start(out, result[:])

@@ -11,6 +11,8 @@ V = 384
 N = RELATIONS * V
 BLOCKS = K // P
 COLS = V // 16
+BANK = 512
+WARM_UPS = 6
 
 FLOPS = 2 * K * M * N
 
@@ -37,6 +39,12 @@ def tile_gather_matmul_kernel(tc, table, w, r, offs, out):
 
         own = held.tile([M, V], F32, name="own")
         nc.gpsimd.dma_start(own[:], r)
+
+        zeros = held.tile([P, BANK], BF16, name="zeros")
+        nc.vector.memset(zeros[:], 0.0)
+        unread = psum.tile([P, BANK], F32, name="unread")
+        for i in range(WARM_UPS):
+            nc.tensor.matmul(unread[:], zeros[:, :P], zeros[:], start=True, stop=True)
 
         bank = psum.tile([M, V], F32, name="bank")
         for b in range(BLOCKS):

@@ -11,8 +11,7 @@ V = 384
 N = RELATIONS * V
 BLOCKS = K // P
 COLS = V // 16
-BANK = 512
-WARM_UPS = 6
+HALF = S // 2
 
 FLOPS = 2 * K * M * N
 
@@ -26,32 +25,34 @@ def tile_gather_matmul_kernel(tc, table, w, r, offs, out):
         offsets = held.tile([P, N // 16], U16, name="offsets")
         nc.sync.dma_start(offsets[:], offs)
 
+        def load_weight(b, t):
+            weight = held.tile([P, M], BF16, name="weight%d%d" % (b, t))
+            queue = nc.scalar if t % 2 == 0 else nc.sync
+            queue.dma_start(weight[:], w[t, b * P : (b + 1) * P, :])
+            return weight
+
         windows = []
         weights = []
         for b in range(BLOCKS):
             rows = slice(b * P, (b + 1) * P)
+            block_weights = [load_weight(b, 0)]
             window = held.tile([P, S], BF16, name="window%d" % b)
-            nc.sync.dma_start(window[:], table[rows, :])
+            nc.sync.dma_start(window[:, :HALF], table[rows, :HALF])
+            nc.scalar.dma_start(window[:, HALF:], table[rows, HALF:])
+            for t in range(1, RELATIONS):
+                block_weights.append(load_weight(b, t))
             windows.append(window)
-            weight = held.tile([P, RELATIONS, M], BF16, name="weight%d" % b)
-            nc.scalar.dma_start(weight[:], w[:, rows, :].rearrange("t p m -> p t m"))
-            weights.append(weight)
+            weights.append(block_weights)
 
         own = held.tile([M, V], F32, name="own")
-        nc.gpsimd.dma_start(own[:], r)
-
-        zeros = held.tile([P, BANK], BF16, name="zeros")
-        nc.vector.memset(zeros[:], 0.0)
-        unread = psum.tile([P, BANK], F32, name="unread")
-        for i in range(WARM_UPS):
-            nc.tensor.matmul(unread[:], zeros[:, :P], zeros[:], start=True, stop=True)
+        nc.scalar.dma_start(own[:], r)
 
         bank = psum.tile([M, V], F32, name="bank")
         for b in range(BLOCKS):
             for t in range(RELATIONS):
                 nc.tensor.matmul(
                     bank[:],
-                    weights[b][:, t, :],
+                    weights[b][t][:],
                     windows[b][:].indirect(offsets[:, t * COLS : (t + 1) * COLS]),
                     start=(b == 0 and t == 0),
                     stop=(b == BLOCKS - 1 and t == RELATIONS - 1),

@@ -12,6 +12,7 @@ N = RELATIONS * V
 BLOCKS = K // P
 COLS = V // 16
 HALF = S // 2
+ALIGN = 256
 
 FLOPS = 2 * K * M * N
 
@@ -22,11 +23,11 @@ def tile_gather_matmul_kernel(tc, table, w, r, offs, out):
         tc.tile_pool(name="held", bufs=1) as held,
         tc.psum_pool(name="psum", bufs=1) as psum,
     ):
-        offsets = held.tile([P, N // 16], U16, name="offsets")
+        offsets = held.tile([P, N // 16], U16, name="offsets", align_bytes=ALIGN)
         nc.sync.dma_start(offsets[:], offs)
 
         def load_weight(b, t):
-            weight = held.tile([P, M], BF16, name="weight%d%d" % (b, t))
+            weight = held.tile([P, M], BF16, name="weight%d%d" % (b, t), align_bytes=ALIGN)
             queue = nc.scalar if t % 2 == 0 else nc.sync
             queue.dma_start(weight[:], w[t, b * P : (b + 1) * P, :])
             return weight
@@ -36,7 +37,7 @@ def tile_gather_matmul_kernel(tc, table, w, r, offs, out):
         for b in range(BLOCKS):
             rows = slice(b * P, (b + 1) * P)
             block_weights = [load_weight(b, 0)]
-            window = held.tile([P, S], BF16, name="window%d" % b)
+            window = held.tile([P, S], BF16, name="window%d" % b, align_bytes=ALIGN)
             nc.sync.dma_start(window[:, :HALF], table[rows, :HALF])
             nc.scalar.dma_start(window[:, HALF:], table[rows, HALF:])
             for t in range(1, RELATIONS):
@@ -44,7 +45,7 @@ def tile_gather_matmul_kernel(tc, table, w, r, offs, out):
             windows.append(window)
             weights.append(block_weights)
 
-        own = held.tile([M, V], F32, name="own")
+        own = held.tile([M, V], F32, name="own", align_bytes=ALIGN)
         nc.scalar.dma_start(own[:], r)
 
         bank = psum.tile([M, V], F32, name="bank")
@@ -58,6 +59,6 @@ def tile_gather_matmul_kernel(tc, table, w, r, offs, out):
                     stop=(b == BLOCKS - 1 and t == RELATIONS - 1),
                 )
 
-        result = held.tile([M, V], F32, name="result")
+        result = held.tile([M, V], F32, name="result", align_bytes=ALIGN)
         nc.vector.tensor_tensor(result[:], bank[:], own[:], mybir.AluOpType.add)
         nc.sync.dma_start(out, result[:])

@@ -12,6 +12,7 @@ N = RELATIONS * V
 BLOCKS = K // P
 COLS = V // 16
 HALF = S // 2
+LAST = 128
 ALIGN = 256
 
 FLOPS = 2 * K * M * N
@@ -60,5 +61,6 @@ def tile_gather_matmul_kernel(tc, table, w, r, offs, out):
                 )
 
         result = held.tile([M, V], F32, name="result", align_bytes=ALIGN)
-        nc.vector.tensor_tensor(result[:], bank[:], own[:], mybir.AluOpType.add)
-        nc.sync.dma_start(out, result[:])
+        for cols, queue in ((slice(0, V - LAST), nc.scalar), (slice(V - LAST, V), nc.sync)):
+            nc.vector.tensor_tensor(result[:, cols], bank[:, cols], own[:, cols], mybir.AluOpType.add)
+            queue.dma_start(out[:, cols], result[:, cols])

@@ -12,7 +12,7 @@ N = RELATIONS * V
 BLOCKS = K // P
 COLS = V // 16
 HALF = S // 2
-LAST = 128
+LAST = V // 2
 ALIGN = 256
 
 FLOPS = 2 * K * M * N

@@ -11,7 +11,6 @@ V = 384
 N = RELATIONS * V
 BLOCKS = K // P
 COLS = V // 16
-HALF = S // 2
 LAST = V // 2
 ALIGN = 256
 
@@ -39,8 +38,10 @@ def tile_gather_matmul_kernel(tc, table, w, r, offs, out):
             rows = slice(b * P, (b + 1) * P)
             block_weights = [load_weight(b, 0)]
             window = held.tile([P, S], BF16, name="window%d" % b, align_bytes=ALIGN)
-            nc.sync.dma_start(window[:, :HALF], table[rows, :HALF])
-            nc.scalar.dma_start(window[:, HALF:], table[rows, HALF:])
+            halves = window[:].rearrange("(q two) s -> q two s", two=2)
+            sources = table[rows, :].rearrange("(q two) s -> q two s", two=2)
+            nc.sync.dma_start(halves[:, 0, :], sources[:, 0, :])
+            nc.scalar.dma_start(halves[:, 1, :], sources[:, 1, :])
             for t in range(1, RELATIONS):
                 block_weights.append(load_weight(b, t))
             windows.append(window)

import concourse.mybir as mybir

BF16, F32, U16 = mybir.dt.bfloat16, mybir.dt.float32, mybir.dt.uint16

P = 128
S = 2048
K = 256
M = 128
RELATIONS = 4
V = 384
N = RELATIONS * V
BLOCKS = K // P
COLS = V // 16
LAST = V // 2
ALIGN = 256

FLOPS = 2 * K * M * N


def tile_gather_matmul_kernel(tc, table, w, r, offs, out):
    nc = tc.nc
    with (
        tc.tile_pool(name="held", bufs=1) as held,
        tc.psum_pool(name="psum", bufs=1) as psum,
    ):
        offsets = held.tile([P, N // 16], U16, name="offsets", align_bytes=ALIGN)
        nc.sync.dma_start(offsets[:], offs)

        def load_weight(b, t):
            weight = held.tile([P, M], BF16, name="weight%d%d" % (b, t), align_bytes=ALIGN)
            queue = nc.scalar if t % 2 == 0 else nc.sync
            queue.dma_start(weight[:], w[t, b * P : (b + 1) * P, :])
            return weight

        windows = []
        weights = []
        for b in range(BLOCKS):
            rows = slice(b * P, (b + 1) * P)
            block_weights = [load_weight(b, 0)]
            window = held.tile([P, S], BF16, name="window%d" % b, align_bytes=ALIGN)
            halves = window[:].rearrange("(q two) s -> q two s", two=2)
            sources = table[rows, :].rearrange("(q two) s -> q two s", two=2)
            nc.sync.dma_start(halves[:, 0, :], sources[:, 0, :])
            nc.scalar.dma_start(halves[:, 1, :], sources[:, 1, :])
            for t in range(1, RELATIONS):
                block_weights.append(load_weight(b, t))
            windows.append(window)
            weights.append(block_weights)

        own = held.tile([M, V], F32, name="own", align_bytes=ALIGN)
        nc.scalar.dma_start(own[:], r)

        bank = psum.tile([M, V], F32, name="bank")
        for b in range(BLOCKS):
            for t in range(RELATIONS):
                nc.tensor.matmul(
                    bank[:],
                    weights[b][t][:],
                    windows[b][:].indirect(offsets[:, t * COLS : (t + 1) * COLS]),
                    start=(b == 0 and t == 0),
                    stop=(b == BLOCKS - 1 and t == RELATIONS - 1),
                )

        result = held.tile([M, V], F32, name="result", align_bytes=ALIGN)
        for cols, queue in ((slice(0, V - LAST), nc.scalar), (slice(V - LAST, V), nc.sync)):
            nc.vector.tensor_tensor(result[:, cols], bank[:, cols], own[:, cols], mybir.AluOpType.add)
            queue.dma_start(out[:, cols], result[:, cols])
